import numpy as np
import ml_dtypes


def mxq(x, axis, fmt="e4m3"):
    dtype, down = {"e4m3": (ml_dtypes.float8_e4m3fn, 7), "e5m2": (ml_dtypes.float8_e5m2, 14)}[fmt]
    v = np.moveaxis(np.asarray(x, np.float32).astype(ml_dtypes.bfloat16).astype(np.float64), axis, -1)
    blocks = v.reshape(v.shape[:-1] + (-1, 32))
    amax = np.abs(blocks).max(-1, keepdims=True)
    byte = np.maximum(np.where(amax > 0, np.frexp(amax)[1] - 1 + 127, 0) - down, 1)
    scale = np.exp2(byte - 127.0)
    codes = (blocks / scale).astype(np.float32).astype(dtype).astype(np.float64)
    return np.moveaxis((codes * scale).reshape(v.shape), -1, axis)


WIDE = False


def mx_kscale(k):
    if not WIDE:
        return np.ones(k)
    levels = np.array([10, -10, 5, -5, 0])
    if k % 512:
        return np.exp2(np.random.permutation(np.resize(levels, k // 32))).repeat(32)
    a = np.empty((k // 512, 16))
    for p in range(k // 512):
        a[p, :8] = np.random.permutation(np.resize(levels, 8))
        for g in range(8):
            far = levels[np.abs(levels - a[p, g]) >= 10]
            a[p, g + 8] = far[np.random.randint(len(far))]
    return np.exp2(a.ravel()).repeat(32)


def f64(x):
    return np.asarray(x).astype(np.float64)


def striped(idx):
    return np.tile(idx.reshape(-1, 16).T, (8, 1)).astype(np.uint16)


def unstriped(offs):
    return offs[:16].T.reshape(-1).astype(np.int64)


E2M1 = np.array([0.0, 0.5, 1.0, 1.5, 2.0, 3.0, 4.0, 6.0, -0.0, -0.5, -1.0, -1.5, -2.0, -3.0, -4.0, -6.0])


def pack_weight(w, fmt):
    k, n = w.shape
    w = f64(np.asarray(w, np.float32).astype(ml_dtypes.bfloat16)).reshape(k // 32, 32, n)
    amax = np.abs(w).max(1)
    if fmt == "e4m3":
        byte = np.frexp(amax)[1] - 1 + 127 - 7
    else:
        mant, ex = np.frexp(amax / 6.0)
        byte = np.where(mant > 0.5, ex, ex - 1) + 127
    byte = np.clip(np.where(amax > 0, byte, 1), 1, 254)
    scaled = (w * np.exp2(127.0 - byte)[:, None, :]).reshape(k, n).astype(np.float32)
    by_word = np.ascontiguousarray(scaled.reshape(k // 512, 128, 4, n).transpose(0, 1, 3, 2))
    if fmt == "e4m3":
        words = by_word.astype(ml_dtypes.float8_e4m3fn).view(np.uint8)
    else:
        c = by_word.astype(ml_dtypes.float4_e2m1fn).view(np.uint8) & 0xF
        words = (c[..., 0::2] | (c[..., 1::2] << 4)).reshape(k // 512, 128, 2 * n)
    return np.ascontiguousarray(words), np.ascontiguousarray(byte.astype(np.uint8).reshape(k // 512, 16, n))


def unpack_weight(words, scales, fmt):
    g, _, n = scales.shape
    words = np.ascontiguousarray(words).reshape(g, 128, n, -1)
    if fmt == "e4m3":
        vals = words.view(ml_dtypes.float8_e4m3fn).astype(np.float64)
    else:
        nib = np.empty((g, 128, n, 4), np.uint8)
        nib[..., 0::2] = words & 0xF
        nib[..., 1::2] = words >> 4
        vals = E2M1[nib]
    vals = vals * np.repeat(np.exp2(scales.astype(np.float64) - 127.0), 8, axis=1)[..., None]
    return vals.transpose(0, 1, 3, 2).reshape(g * 512, n)


def relu2(v):
    return np.maximum(v, 0.0) ** 2


K, T, E, C, N = 1536, 512, 12, 128, 128
TOP = 3


def by_expert(wq, xq):
    return np.concatenate([wq[e].T @ xq[:, e * C:(e + 1) * C] for e in range(E)], axis=1)


def setup_inputs():
    n = np.random.standard_normal
    s = mx_kscale(K)[:, None]
    deal = np.repeat(np.arange(E), C).reshape(TOP, T)[:, np.random.permutation(T)]
    deal = np.take_along_axis(deal, np.argsort(np.random.rand(TOP, T), axis=0), axis=0)
    for _ in range(8):
        s_, t_ = np.random.permutation(T).reshape(2, -1); r = np.random.randint(TOP, size=T // 2); x, y = deal[r, s_].copy(), deal[r, t_].copy()
        ok = ~((deal[:, s_] == y).any(0) | (deal[:, t_] == x).any(0)); deal[r[ok], s_[ok]] = y[ok]; deal[r[ok], t_[ok]] = x[ok]
    order = np.lexsort((np.random.rand(TOP * T), deal.reshape(-1)))
    slot_token = order % T; pos = np.empty(TOP * T, np.int64); pos[order] = np.arange(TOP * T); pos = pos.reshape(TOP, T)
    g = np.random.uniform(0.5, 1.5, (TOP, T)); g = g / g.sum(0)
    x = pack_weight(n((K, T)) * s, "e4m3")
    return {
        "x_words": x[0],
        "x_scales": x[1],
        "w": (n((E, K, N)) / np.sqrt(K) / s[None]).astype(np.float32),
        "b": (0.3 * n((N, E))).astype(np.float32),
        "gate": np.stack([np.tile(r, (N, 1)) for r in g]).astype(np.float32),
        "offs": striped(slot_token),
        "pos1": striped(pos[0]),
        "pos2": striped(pos[1]),
        "pos3": striped(pos[2]),
    }


def reference(x_words, x_scales, w, b, gate, offs, pos1, pos2, pos3):
    idx = unstriped(offs)
    xq = unpack_weight(x_words, x_scales, "e4m3")[:, idx]
    y = by_expert(mxq(f64(w), 1, "e4m3"), xq)
    y = relu2(y + np.repeat(f64(b), C, axis=1))
    return sum(f64(gate[r]) * y[:, unstriped(p)] for r, p in enumerate((pos1, pos2, pos3)))

@@ -1,0 +1,152 @@
+from contextlib import ExitStack
+
+import concourse.mybir as mybir
+
+K, T, E, C, N = 1536, 512, 12, 128, 128
+TOP = 3
+FLOPS = 2 * K * N * E * C
+
+F32 = mybir.dt.float32
+BF16 = mybir.dt.bfloat16
+I32 = mybir.dt.int32
+U32 = mybir.dt.uint32
+U16 = mybir.dt.uint16
+U8 = mybir.dt.uint8
+FP8X4 = mybir.dt.float8_e4m3fn_x4
+ACT = mybir.ActivationFunctionType
+ALU = mybir.AluOpType
+
+P = 128
+PACK = 4
+PASSES = K // (P * PACK)
+SLOTS = E * C
+GATHER = 384
+PER_COL = 16
+BY_PASS = tuple(range(12))
+SCALES_AFTER = 2
+BIAS_AFTER = 8
+ON_VECTOR = ((9, 0), (9, 1), (9, 2), (10, 0), (10, 1), (10, 2), (11, 0), (11, 2))
+BANK_OF = [(0, 0), (0, 1), (1, 0), (1, 1), (2, 0), (2, 1), (3, 0), (3, 1), (4, 0), (5, 0), (6, 0), (7, 0)]
+SQUARES = ((0, 4), (4, 8), (8, 10), (10, 11), (11, 12))
+PARTS = ((0, 256), (256, 512))
+
+
+def tile_moe_pkd_lin_relu2_kernel(tc, x_words, x_scales, w, b, gate, offs, pos1, pos2, pos3, out):
+    nc = tc.nc
+    with ExitStack() as ctx:
+        keep = ctx.enter_context(tc.tile_pool(name="keep", bufs=1))
+        psum = ctx.enter_context(tc.psum_pool(name="psum", bufs=1))
+
+        offs_sb = keep.tile([P, SLOTS // PER_COL], U16, name="offs_sb")
+        pos_sb = [keep.tile([P, T // PER_COL], U16, name=f"pos_sb{r}") for r in range(TOP)]
+        xw = [keep.tile([P, T], U32, name=f"xw{a}", align_bytes=64) for a in range(PASSES)]
+        xs = keep.tile([P, T], U8, name="xs", align_bytes=64)
+        bias = keep.tile([P, E], F32, name="bias")
+        gates = [keep.tile([P, T], F32, name=f"gate{r}") for r in range(TOP)]
+
+        nc.vector.memset(xs[:].bitcast(I32), 0)
+
+        raw = {}
+
+        def load_w(e, a0, a1):
+            t = keep.tile([P, a1 - a0, PACK * N], F32, name=f"raw{e}_{a0}")
+            nc.sync.dma_start(out=t[:], in_=w[e].rearrange("(g p j) n -> p g (j n)", p=P, j=PACK)[:, a0:a1, :])
+            raw[(e, a0)] = (t, a1 - a0)
+
+        def load_x(a):
+            nc.sync.dma_start(out=xw[a][:].bitcast(I32), in_=x_words[a].rearrange("p t r -> p (t r)").bitcast(I32))
+
+        nc.sync.dma_start(offs_sb[:], offs)
+        for e in range(E):
+            if e < PASSES:
+                load_x(e)
+            if e in BY_PASS:
+                for a in range(PASSES):
+                    load_w(e, a, a + 1)
+            else:
+                load_w(e, 0, PASSES)
+            if e == SCALES_AFTER:
+                for q in range(4):
+                    nc.sync.dma_start(out=xs[32 * q : 32 * q + 4 * PASSES, :].bitcast(I32), in_=x_scales[:, 4 * q : 4 * q + 4, :].bitcast(I32))
+            if e == BIAS_AFTER:
+                for r, pos in enumerate((pos1, pos2, pos3)):
+                    nc.sync.dma_start(pos_sb[r][:], pos)
+                nc.sync.dma_start(out=bias[:], in_=b)
+        for r in range(TOP):
+            nc.sync.dma_start(out=gates[r][:], in_=gate[r])
+
+        gw = {}
+        gs = {}
+        for a in range(PASSES):
+            for h in range(SLOTS // GATHER):
+                cols = offs_sb[:, h * GATHER // PER_COL : (h + 1) * GATHER // PER_COL]
+                gw[(h, a)] = keep.tile([P, GATHER], U32, name=f"gw{h}_{a}", align_bytes=64)
+                nc.vector.tensor_copy(out=gw[(h, a)][:], in_=xw[a][:].indirect(cols))
+        for h in range(SLOTS // GATHER):
+            cols = offs_sb[:, h * GATHER // PER_COL : (h + 1) * GATHER // PER_COL]
+            gs[h] = keep.tile([P, GATHER], U8, name=f"gs{h}", align_bytes=64)
+            nc.vector.tensor_copy(out=gs[h][:], in_=xs[:].indirect(cols))
+
+        y = keep.tile([P, SLOTS], F32, name="y")
+        banks = [psum.tile([P, 512], F32, name=f"bank{i}") for i in range(8)]
+
+        wb = [keep.tile([P, PASSES, N * PACK], BF16, name=f"wb{e}", align_bytes=64) for e in range(E)]
+        for e in range(E):
+            for a0 in range(PASSES):
+                if (e, a0) not in raw:
+                    continue
+                t, count = raw[(e, a0)]
+                src = t[:].rearrange("p g (j c i) -> p g c j i", j=PACK, i=4)
+                dst = wb[e][:, a0 : a0 + count, :].rearrange("p g (c i j) -> p g c j i", j=PACK, i=4)
+                if (e, a0) == (0, 0):
+                    nc.scalar.activation(out=dst[:, 0], in_=src[:, 0], func=ACT.Copy)
+                elif (e, a0) in ON_VECTOR:
+                    for g in range(count):
+                        nc.vector.tensor_copy(out=dst[:, g], in_=src[:, g])
+                else:
+                    nc.scalar.copy(out=dst, in_=src)
+
+        accs = []
+        for e in range(E):
+            codes = keep.tile([P, PASSES * N], U32, name=f"codes{e}", align_bytes=64)
+            scales = keep.tile([P, PASSES * N], U8, name=f"scales{e}", align_bytes=64)
+            flat = wb[e][:].rearrange("p g m -> p (g m)")
+            for a0, a1 in ((0, 2), (2, 3)):
+                nc.vector.quantize_mx(
+                    out=codes[:, a0 * N : a1 * N].bitcast(FP8X4),
+                    scales=scales[:, a0 * N : a1 * N],
+                    in_=flat[:, a0 * N * PACK : a1 * N * PACK],
+                )
+            bank, place = BANK_OF[e]
+            acc = banks[bank][:, place * C : (place + 1) * C]
+            h, c0 = divmod(e * C, GATHER)
+            for a in range(PASSES):
+                nc.tensor.matmul_mx(
+                    out=acc,
+                    lhsT=codes[:, a * N : (a + 1) * N].bitcast(FP8X4),
+                    lhsT_scale=scales[:, a * N : (a + 1) * N],
+                    rhs=gw[(h, a)][:, c0 : c0 + C].bitcast(FP8X4),
+                    rhs_scale=gs[h][4 * a : P, c0 : c0 + C],
+                    start=(a == 0),
+                    stop=(a == PASSES - 1),
+                )
+            accs.append(acc)
+
+        rel = keep.tile([P, SLOTS], F32, name="rel")
+        for e0, e1 in SQUARES:
+            for e in range(e0, e1):
+                nc.scalar.activation(out=rel[:, e * C : (e + 1) * C], in_=accs[e], func=ACT.Relu, bias=bias[:, e : e + 1])
+            nc.scalar.activation(out=y[:, e0 * C : e1 * C], in_=rel[:, e0 * C : e1 * C], func=ACT.Square)
+
+        for t0, t1 in PARTS:
+            width = t1 - t0
+            terms = []
+            for r in range(TOP):
+                term = keep.tile([P, width], F32, name=f"term{t0}_{r}")
+                nc.vector.tensor_tensor(out=term[:], in0=y[:].indirect(pos_sb[r][:, t0 // PER_COL : t1 // PER_COL]), in1=gates[r][:, t0:t1], op=ALU.mult)
+                terms.append(term)
+            two = keep.tile([P, width], F32, name=f"two{t0}")
+            nc.vector.tensor_tensor(out=two[:], in0=terms[0][:], in1=terms[1][:], op=ALU.add)
+            res = keep.tile([P, width], F32, name=f"res{t0}")
+            nc.vector.tensor_tensor(out=res[:], in0=two[:], in1=terms[2][:], op=ALU.add)
+            nc.sync.dma_start(out=out[:, t0:t1], in_=res[:])

@@ -22,13 +22,14 @@ PASSES = K // (P * PACK)
 SLOTS = E * C
 GATHER = 384
 PER_COL = 16
-BY_PASS = tuple(range(12))
+BY_PASS = (11,)
 SCALES_AFTER = 2
 BIAS_AFTER = 8
-ON_VECTOR = ((9, 0), (9, 1), (9, 2), (10, 0), (10, 1), (10, 2), (11, 0), (11, 2))
+ON_VECTOR = ((9, 0), (10, 0), (11, 0), (11, 2))
 BANK_OF = [(0, 0), (0, 1), (1, 0), (1, 1), (2, 0), (2, 1), (3, 0), (3, 1), (4, 0), (5, 0), (6, 0), (7, 0)]
 SQUARES = ((0, 4), (4, 8), (8, 10), (10, 11), (11, 12))
-PARTS = ((0, 256), (256, 512))
+CUT = 384
+SHARE = 16
 
 
 def tile_moe_pkd_lin_relu2_kernel(tc, x_words, x_scales, w, b, gate, offs, pos1, pos2, pos3, out):
@@ -39,10 +40,12 @@ def tile_moe_pkd_lin_relu2_kernel(tc, x_words, x_scales, w, b, gate, offs, pos1,
 
         offs_sb = keep.tile([P, SLOTS // PER_COL], U16, name="offs_sb")
         pos_sb = [keep.tile([P, T // PER_COL], U16, name=f"pos_sb{r}") for r in range(TOP)]
-        xw = [keep.tile([P, T], U32, name=f"xw{a}", align_bytes=64) for a in range(PASSES)]
+        xw0 = keep.tile([P, T], U32, name="xw0", align_bytes=64)
+        xw12 = keep.tile([P, PASSES - 1, T], U32, name="xw12", align_bytes=64)
+        xw = [xw0[:], xw12[:, 0, :], xw12[:, 1, :]]
         xs = keep.tile([P, T], U8, name="xs", align_bytes=64)
         bias = keep.tile([P, E], F32, name="bias")
-        gates = [keep.tile([P, T], F32, name=f"gate{r}") for r in range(TOP)]
+        gates = keep.tile([P, TOP, T], F32, name="gates")
 
         nc.vector.memset(xs[:].bitcast(I32), 0)
 
@@ -53,13 +56,14 @@ def tile_moe_pkd_lin_relu2_kernel(tc, x_words, x_scales, w, b, gate, offs, pos1,
             nc.sync.dma_start(out=t[:], in_=w[e].rearrange("(g p j) n -> p g (j n)", p=P, j=PACK)[:, a0:a1, :])
             raw[(e, a0)] = (t, a1 - a0)
 
-        def load_x(a):
-            nc.sync.dma_start(out=xw[a][:].bitcast(I32), in_=x_words[a].rearrange("p t r -> p (t r)").bitcast(I32))
+        x_i32 = x_words.rearrange("a p t r -> p a (t r)").bitcast(I32)
 
         nc.sync.dma_start(offs_sb[:], offs)
         for e in range(E):
-            if e < PASSES:
-                load_x(e)
+            if e == 0:
+                nc.sync.dma_start(out=xw0[:].bitcast(I32), in_=x_i32[:, 0, :])
+            if e == 1:
+                nc.sync.dma_start(out=xw12[:].bitcast(I32), in_=x_i32[:, 1:, :])
             if e in BY_PASS:
                 for a in range(PASSES):
                     load_w(e, a, a + 1)
@@ -69,11 +73,11 @@ def tile_moe_pkd_lin_relu2_kernel(tc, x_words, x_scales, w, b, gate, offs, pos1,
                 for q in range(4):
                     nc.sync.dma_start(out=xs[32 * q : 32 * q + 4 * PASSES, :].bitcast(I32), in_=x_scales[:, 4 * q : 4 * q + 4, :].bitcast(I32))
             if e == BIAS_AFTER:
-                for r, pos in enumerate((pos1, pos2, pos3)):
-                    nc.sync.dma_start(pos_sb[r][:], pos)
                 nc.sync.dma_start(out=bias[:], in_=b)
+        for r, pos in enumerate((pos1, pos2, pos3)):
+            nc.sync.dma_start(pos_sb[r][:], pos)
         for r in range(TOP):
-            nc.sync.dma_start(out=gates[r][:], in_=gate[r])
+            nc.sync.dma_start(out=gates[:, r, :], in_=gate[r])
 
         gw = {}
         gs = {}
@@ -81,7 +85,7 @@ def tile_moe_pkd_lin_relu2_kernel(tc, x_words, x_scales, w, b, gate, offs, pos1,
             for h in range(SLOTS // GATHER):
                 cols = offs_sb[:, h * GATHER // PER_COL : (h + 1) * GATHER // PER_COL]
                 gw[(h, a)] = keep.tile([P, GATHER], U32, name=f"gw{h}_{a}", align_bytes=64)
-                nc.vector.tensor_copy(out=gw[(h, a)][:], in_=xw[a][:].indirect(cols))
+                nc.vector.tensor_copy(out=gw[(h, a)][:], in_=xw[a].indirect(cols))
         for h in range(SLOTS // GATHER):
             cols = offs_sb[:, h * GATHER // PER_COL : (h + 1) * GATHER // PER_COL]
             gs[h] = keep.tile([P, GATHER], U8, name=f"gs{h}", align_bytes=64)
@@ -98,8 +102,12 @@ def tile_moe_pkd_lin_relu2_kernel(tc, x_words, x_scales, w, b, gate, offs, pos1,
                 t, count = raw[(e, a0)]
                 src = t[:].rearrange("p g (j c i) -> p g c j i", j=PACK, i=4)
                 dst = wb[e][:, a0 : a0 + count, :].rearrange("p g (c i j) -> p g c j i", j=PACK, i=4)
-                if (e, a0) == (0, 0):
-                    nc.scalar.activation(out=dst[:, 0], in_=src[:, 0], func=ACT.Copy)
+                if e == 0:
+                    for g in range(count):
+                        nc.scalar.activation(out=dst[:, g], in_=src[:, g], func=ACT.Copy)
+                elif (e, a0) == (E - 1, PASSES - 1):
+                    nc.vector.tensor_copy(out=dst[:, 0, :SHARE], in_=src[:, 0, :SHARE])
+                    nc.scalar.copy(out=dst[:, 0, SHARE:], in_=src[:, 0, SHARE:])
                 elif (e, a0) in ON_VECTOR:
                     for g in range(count):
                         nc.vector.tensor_copy(out=dst[:, g], in_=src[:, g])
@@ -138,15 +146,22 @@ def tile_moe_pkd_lin_relu2_kernel(tc, x_words, x_scales, w, b, gate, offs, pos1,
                 nc.scalar.activation(out=rel[:, e * C : (e + 1) * C], in_=accs[e], func=ACT.Relu, bias=bias[:, e : e + 1])
             nc.scalar.activation(out=y[:, e0 * C : e1 * C], in_=rel[:, e0 * C : e1 * C], func=ACT.Square)
 
-        for t0, t1 in PARTS:
-            width = t1 - t0
-            terms = []
-            for r in range(TOP):
-                term = keep.tile([P, width], F32, name=f"term{t0}_{r}")
-                nc.vector.tensor_tensor(out=term[:], in0=y[:].indirect(pos_sb[r][:, t0 // PER_COL : t1 // PER_COL]), in1=gates[r][:, t0:t1], op=ALU.mult)
-                terms.append(term)
-            two = keep.tile([P, width], F32, name=f"two{t0}")
-            nc.vector.tensor_tensor(out=two[:], in0=terms[0][:], in1=terms[1][:], op=ALU.add)
-            res = keep.tile([P, width], F32, name=f"res{t0}")
-            nc.vector.tensor_tensor(out=res[:], in0=two[:], in1=terms[2][:], op=ALU.add)
-            nc.sync.dma_start(out=out[:, t0:t1], in_=res[:])
+        def weigh(t0, t1, r):
+            term = keep.tile([P, t1 - t0], F32, name=f"term{t0}_{r}")
+            nc.vector.tensor_tensor(out=term[:], in0=y[:].indirect(pos_sb[r][:, t0 // PER_COL : t1 // PER_COL]), in1=gates[:, r, t0:t1], op=ALU.mult)
+            return term
+
+        def add(left, right, name):
+            total = keep.tile(list(left.shape), F32, name=name)
+            nc.vector.tensor_tensor(out=total[:], in0=left[:], in1=right[:], op=ALU.add)
+            return total
+
+        first = [weigh(0, CUT, r) for r in range(TOP)]
+        first_two = add(first[0], first[1], "first_two")
+        last = [weigh(CUT, T, 0)]
+        first_sum = add(first_two, first[2], "first_sum")
+        nc.sync.dma_start(out=out[:, :CUT], in_=first_sum[:])
+        last.extend(weigh(CUT, T, r) for r in range(1, TOP))
+        last_two = add(last[0], last[1], "last_two")
+        last_sum = add(last_two, last[2], "last_sum")
+        nc.sync.dma_start(out=out[:, CUT:], in_=last_sum[:])

@@ -29,7 +29,7 @@ ON_VECTOR = ((9, 0), (10, 0), (11, 0), (11, 2))
 BANK_OF = [(0, 0), (0, 1), (1, 0), (1, 1), (2, 0), (2, 1), (3, 0), (3, 1), (4, 0), (5, 0), (6, 0), (7, 0)]
 SQUARES = ((0, 4), (4, 8), (8, 10), (10, 11), (11, 12))
 CUT = 384
-SHARE = 16
+SHARE = 32
 
 
 def tile_moe_pkd_lin_relu2_kernel(tc, x_words, x_scales, w, b, gate, offs, pos1, pos2, pos3, out):
@@ -100,8 +100,8 @@ def tile_moe_pkd_lin_relu2_kernel(tc, x_words, x_scales, w, b, gate, offs, pos1,
                 if (e, a0) not in raw:
                     continue
                 t, count = raw[(e, a0)]
-                src = t[:].rearrange("p g (j c i) -> p g c j i", j=PACK, i=4)
-                dst = wb[e][:, a0 : a0 + count, :].rearrange("p g (c i j) -> p g c j i", j=PACK, i=4)
+                src = t[:].rearrange("p g (j c i) -> p g c j i", j=PACK, i=2)
+                dst = wb[e][:, a0 : a0 + count, :].rearrange("p g (c i j) -> p g c j i", j=PACK, i=2)
                 if e == 0:
                     for g in range(count):
                         nc.scalar.activation(out=dst[:, g], in_=src[:, g], func=ACT.Copy)

@@ -1,6 +1,7 @@
 from contextlib import ExitStack
 
 import concourse.mybir as mybir
+from concourse.masks import make_identity
 
 K, T, E, C, N = 1536, 512, 12, 128, 128
 TOP = 3
@@ -25,11 +26,13 @@ PER_COL = 16
 BY_PASS = (11,)
 SCALES_AFTER = 2
 BIAS_AFTER = 8
-ON_VECTOR = ((9, 0), (10, 0), (11, 0), (11, 2))
+ON_VECTOR = ((9, 0), (9, 1), (9, 2), (10, 0), (10, 1), (10, 2), (11, 0), (11, 2))
 BANK_OF = [(0, 0), (0, 1), (1, 0), (1, 1), (2, 0), (2, 1), (3, 0), (3, 1), (4, 0), (5, 0), (6, 0), (7, 0)]
-SQUARES = ((0, 4), (4, 8), (8, 10), (10, 11), (11, 12))
-CUT = 384
-SHARE = 32
+SQUARES = ((0, 4), (4, 8), (8, 10), (10, 11))
+CUT = 256
+
+WINDOW = 2048
+QUANTS = (4, 4, 4, 4, 4, 4, 2, 1, 2, 1, 2, 1, 1, 1, 1)
 
 
 def tile_moe_pkd_lin_relu2_kernel(tc, x_words, x_scales, w, b, gate, offs, pos1, pos2, pos3, out):
@@ -40,14 +43,16 @@ def tile_moe_pkd_lin_relu2_kernel(tc, x_words, x_scales, w, b, gate, offs, pos1,
 
         offs_sb = keep.tile([P, SLOTS // PER_COL], U16, name="offs_sb")
         pos_sb = [keep.tile([P, T // PER_COL], U16, name=f"pos_sb{r}") for r in range(TOP)]
-        xw0 = keep.tile([P, T], U32, name="xw0", align_bytes=64)
-        xw12 = keep.tile([P, PASSES - 1, T], U32, name="xw12", align_bytes=64)
-        xw = [xw0[:], xw12[:, 0, :], xw12[:, 1, :]]
-        xs = keep.tile([P, T], U8, name="xs", align_bytes=64)
+        xw = keep.tile([P, (PASSES - 1) * T + WINDOW], U32, name="xw", align_bytes=64)
+        xw_start = [2 * T, 0, T]
+        xs = keep.tile([P, WINDOW], U8, name="xs", align_bytes=64)
         bias = keep.tile([P, E], F32, name="bias")
-        gates = keep.tile([P, TOP, T], F32, name="gates")
+        gates = {t0: keep.tile([P, TOP, t1 - t0], F32, name=f"gates{t0}") for t0, t1 in ((0, CUT), (CUT, T))}
 
         nc.vector.memset(xs[:].bitcast(I32), 0)
+        nc.vector.memset(xw[:, PASSES * T :].bitcast(I32), 0)
+        ident = keep.tile([P, P], F32, name="ident")
+        make_identity(nc, ident[:])
 
         raw = {}
 
@@ -61,9 +66,9 @@ def tile_moe_pkd_lin_relu2_kernel(tc, x_words, x_scales, w, b, gate, offs, pos1,
         nc.sync.dma_start(offs_sb[:], offs)
         for e in range(E):
             if e == 0:
-                nc.sync.dma_start(out=xw0[:].bitcast(I32), in_=x_i32[:, 0, :])
+                nc.scalar.dma_start(out=xw[:, 2 * T : 3 * T].bitcast(I32), in_=x_i32[:, 0, :])
             if e == 1:
-                nc.sync.dma_start(out=xw12[:].bitcast(I32), in_=x_i32[:, 1:, :])
+                nc.sync.dma_start(out=xw[:, : 2 * T].bitcast(I32).rearrange("p (a t) -> p a t", t=T), in_=x_i32[:, 1:, :])
             if e in BY_PASS:
                 for a in range(PASSES):
                     load_w(e, a, a + 1)
@@ -71,74 +76,70 @@ def tile_moe_pkd_lin_relu2_kernel(tc, x_words, x_scales, w, b, gate, offs, pos1,
                 load_w(e, 0, PASSES)
             if e == SCALES_AFTER:
                 for q in range(4):
-                    nc.sync.dma_start(out=xs[32 * q : 32 * q + 4 * PASSES, :].bitcast(I32), in_=x_scales[:, 4 * q : 4 * q + 4, :].bitcast(I32))
+                    nc.sync.dma_start(out=xs[32 * q : 32 * q + 4 * PASSES, :T].bitcast(I32), in_=x_scales[:, 4 * q : 4 * q + 4, :].bitcast(I32))
             if e == BIAS_AFTER:
                 nc.sync.dma_start(out=bias[:], in_=b)
         for r, pos in enumerate((pos1, pos2, pos3)):
             nc.sync.dma_start(pos_sb[r][:], pos)
-        for r in range(TOP):
-            nc.sync.dma_start(out=gates[:, r, :], in_=gate[r])
+        for t0, t1 in ((0, CUT), (CUT, T)):
+            nc.sync.dma_start(out=gates[t0][:], in_=gate[:, :, t0:t1].rearrange("r n t -> n r t"))
 
-        gw = {}
-        gs = {}
+        gw = []
         for a in range(PASSES):
-            for h in range(SLOTS // GATHER):
-                cols = offs_sb[:, h * GATHER // PER_COL : (h + 1) * GATHER // PER_COL]
-                gw[(h, a)] = keep.tile([P, GATHER], U32, name=f"gw{h}_{a}", align_bytes=64)
-                nc.vector.tensor_copy(out=gw[(h, a)][:], in_=xw[a].indirect(cols))
-        for h in range(SLOTS // GATHER):
-            cols = offs_sb[:, h * GATHER // PER_COL : (h + 1) * GATHER // PER_COL]
-            gs[h] = keep.tile([P, GATHER], U8, name=f"gs{h}", align_bytes=64)
-            nc.vector.tensor_copy(out=gs[h][:], in_=xs[:].indirect(cols))
+            gathered = keep.tile([P, SLOTS], U32, name=f"gw{a}", align_bytes=64)
+            nc.vector.tensor_copy(out=gathered[:], in_=xw[:, xw_start[a] : xw_start[a] + WINDOW].indirect(offs_sb[:]))
+            gw.append(gathered)
+        gs = keep.tile([P, SLOTS], U8, name="gs", align_bytes=64)
+        nc.vector.tensor_copy(out=gs[:], in_=xs[:].indirect(offs_sb[:]))
 
         y = keep.tile([P, SLOTS], F32, name="y")
         banks = [psum.tile([P, 512], F32, name=f"bank{i}") for i in range(8)]
 
-        wb = [keep.tile([P, PASSES, N * PACK], BF16, name=f"wb{e}", align_bytes=64) for e in range(E)]
+        wb = keep.tile([P, E * PASSES, N * PACK], BF16, name="wb", align_bytes=64)
         for e in range(E):
             for a0 in range(PASSES):
                 if (e, a0) not in raw:
                     continue
                 t, count = raw[(e, a0)]
                 src = t[:].rearrange("p g (j c i) -> p g c j i", j=PACK, i=2)
-                dst = wb[e][:, a0 : a0 + count, :].rearrange("p g (c i j) -> p g c j i", j=PACK, i=2)
+                dst = wb[:, e * PASSES + a0 : e * PASSES + a0 + count, :].rearrange("p g (c i j) -> p g c j i", j=PACK, i=2)
+                on_vector = [g for g in range(count) if (e, a0 + g) in ON_VECTOR]
+                for g in on_vector:
+                    nc.vector.tensor_copy(out=dst[:, g], in_=src[:, g])
                 if e == 0:
                     for g in range(count):
                         nc.scalar.activation(out=dst[:, g], in_=src[:, g], func=ACT.Copy)
-                elif (e, a0) == (E - 1, PASSES - 1):
-                    nc.vector.tensor_copy(out=dst[:, 0, :SHARE], in_=src[:, 0, :SHARE])
-                    nc.scalar.copy(out=dst[:, 0, SHARE:], in_=src[:, 0, SHARE:])
-                elif (e, a0) in ON_VECTOR:
-                    for g in range(count):
-                        nc.vector.tensor_copy(out=dst[:, g], in_=src[:, g])
-                else:
-                    nc.scalar.copy(out=dst, in_=src)
+                elif len(on_vector) < count:
+                    nc.scalar.copy(out=dst[:, len(on_vector) :], in_=src[:, len(on_vector) :])
 
+        codes = keep.tile([P, E * PASSES * N], U32, name="codes", align_bytes=64)
+        scales = keep.tile([P, E * PASSES * N], U8, name="scales", align_bytes=64)
+        flat = wb[:].rearrange("p g m -> p (g m)")
         accs = []
-        for e in range(E):
-            codes = keep.tile([P, PASSES * N], U32, name=f"codes{e}", align_bytes=64)
-            scales = keep.tile([P, PASSES * N], U8, name=f"scales{e}", align_bytes=64)
-            flat = wb[e][:].rearrange("p g m -> p (g m)")
-            for a0, a1 in ((0, 2), (2, 3)):
-                nc.vector.quantize_mx(
-                    out=codes[:, a0 * N : a1 * N].bitcast(FP8X4),
-                    scales=scales[:, a0 * N : a1 * N],
-                    in_=flat[:, a0 * N * PACK : a1 * N * PACK],
-                )
-            bank, place = BANK_OF[e]
-            acc = banks[bank][:, place * C : (place + 1) * C]
-            h, c0 = divmod(e * C, GATHER)
-            for a in range(PASSES):
+        u0 = 0
+        for width in QUANTS:
+            u1 = u0 + width
+            nc.vector.quantize_mx(
+                out=codes[:, u0 * N : u1 * N].bitcast(FP8X4),
+                scales=scales[:, u0 * N : u1 * N],
+                in_=flat[:, u0 * N * PACK : u1 * N * PACK],
+            )
+            for u in range(u0, u1):
+                e, a = divmod(u, PASSES)
+                bank, place = BANK_OF[e]
+                acc = banks[bank][:, place * C : (place + 1) * C]
                 nc.tensor.matmul_mx(
                     out=acc,
-                    lhsT=codes[:, a * N : (a + 1) * N].bitcast(FP8X4),
-                    lhsT_scale=scales[:, a * N : (a + 1) * N],
-                    rhs=gw[(h, a)][:, c0 : c0 + C].bitcast(FP8X4),
-                    rhs_scale=gs[h][4 * a : P, c0 : c0 + C],
+                    lhsT=codes[:, u * N : (u + 1) * N].bitcast(FP8X4),
+                    lhsT_scale=scales[:, u * N : (u + 1) * N],
+                    rhs=gw[a][:, e * C : (e + 1) * C].bitcast(FP8X4),
+                    rhs_scale=gs[4 * a : P, e * C : (e + 1) * C],
                     start=(a == 0),
                     stop=(a == PASSES - 1),
                 )
-            accs.append(acc)
+                if a == 0:
+                    accs.append(acc)
+            u0 = u1
 
         rel = keep.tile([P, SLOTS], F32, name="rel")
         for e0, e1 in SQUARES:
@@ -146,9 +147,13 @@ def tile_moe_pkd_lin_relu2_kernel(tc, x_words, x_scales, w, b, gate, offs, pos1,
                 nc.scalar.activation(out=rel[:, e * C : (e + 1) * C], in_=accs[e], func=ACT.Relu, bias=bias[:, e : e + 1])
             nc.scalar.activation(out=y[:, e0 * C : e1 * C], in_=rel[:, e0 * C : e1 * C], func=ACT.Square)
 
+        cols = slice((E - 1) * C, E * C)
+        nc.vector.tensor_scalar(out=rel[:, cols], in0=accs[E - 1], scalar1=bias[:, E - 1 :], scalar2=0.0, op0=ALU.add, op1=ALU.max)
+        nc.vector.tensor_tensor(out=y[:, cols], in0=rel[:, cols], in1=rel[:, cols], op=ALU.mult)
+
         def weigh(t0, t1, r):
             term = keep.tile([P, t1 - t0], F32, name=f"term{t0}_{r}")
-            nc.vector.tensor_tensor(out=term[:], in0=y[:].indirect(pos_sb[r][:, t0 // PER_COL : t1 // PER_COL]), in1=gates[:, r, t0:t1], op=ALU.mult)
+            nc.vector.tensor_tensor(out=term[:], in0=y[:].indirect(pos_sb[r][:, t0 // PER_COL : t1 // PER_COL]), in1=gates[t0][:, r, :], op=ALU.mult)
             return term
 
         def add(left, right, name):
@@ -157,11 +162,19 @@ def tile_moe_pkd_lin_relu2_kernel(tc, x_words, x_scales, w, b, gate, offs, pos1,
             return total
 
         first = [weigh(0, CUT, r) for r in range(TOP)]
-        first_two = add(first[0], first[1], "first_two")
-        last = [weigh(CUT, T, 0)]
-        first_sum = add(first_two, first[2], "first_sum")
+        turned = keep.tile([P, CUT], F32, name="turned")
+        first_sum = keep.tile([P, CUT], F32, name="first_sum")
+        blocks = [slice(t0, t0 + P) for t0 in range(0, CUT, P)]
+        for r in range(TOP):
+            for i, cols in enumerate(blocks):
+                nc.tensor.matmul(banks[i][:, :P], lhsT=first[r][:, cols], rhs=ident[:], is_transpose=True, start=(r == 0), stop=(r == TOP - 1))
+        for i, cols in enumerate(blocks):
+            nc.scalar.copy(out=turned[:, cols], in_=banks[i][:, :P])
+            nc.tensor.transpose(banks[len(blocks) + i][:, :P], turned[:, cols], ident[:])
+        for i, cols in enumerate(blocks):
+            nc.scalar.copy(out=first_sum[:, cols], in_=banks[len(blocks) + i][:, :P])
         nc.sync.dma_start(out=out[:, :CUT], in_=first_sum[:])
-        last.extend(weigh(CUT, T, r) for r in range(1, TOP))
+        last = [weigh(CUT, T, r) for r in range(TOP)]
         last_two = add(last[0], last[1], "last_two")
         last_sum = add(last_two, last[2], "last_sum")
         nc.sync.dma_start(out=out[:, CUT:], in_=last_sum[:])

from contextlib import ExitStack

import concourse.mybir as mybir
from concourse.masks import make_identity

K, T, E, C, N = 1536, 512, 12, 128, 128
TOP = 3
FLOPS = 2 * K * N * E * C

F32 = mybir.dt.float32
BF16 = mybir.dt.bfloat16
I32 = mybir.dt.int32
U32 = mybir.dt.uint32
U16 = mybir.dt.uint16
U8 = mybir.dt.uint8
FP8X4 = mybir.dt.float8_e4m3fn_x4
ACT = mybir.ActivationFunctionType
ALU = mybir.AluOpType

P = 128
PACK = 4
PASSES = K // (P * PACK)
SLOTS = E * C
GATHER = 384
PER_COL = 16
BY_PASS = (11,)
SCALES_AFTER = 2
BIAS_AFTER = 8
ON_VECTOR = ((9, 0), (9, 1), (9, 2), (10, 0), (10, 1), (10, 2), (11, 0), (11, 2))
BANK_OF = [(0, 0), (0, 1), (1, 0), (1, 1), (2, 0), (2, 1), (3, 0), (3, 1), (4, 0), (5, 0), (6, 0), (7, 0)]
SQUARES = ((0, 4), (4, 8), (8, 10), (10, 11))
CUT = 256

WINDOW = 2048
QUANTS = (4, 4, 4, 4, 4, 4, 2, 1, 2, 1, 2, 1, 1, 1, 1)


def tile_moe_pkd_lin_relu2_kernel(tc, x_words, x_scales, w, b, gate, offs, pos1, pos2, pos3, out):
    nc = tc.nc
    with ExitStack() as ctx:
        keep = ctx.enter_context(tc.tile_pool(name="keep", bufs=1))
        psum = ctx.enter_context(tc.psum_pool(name="psum", bufs=1))

        offs_sb = keep.tile([P, SLOTS // PER_COL], U16, name="offs_sb")
        pos_sb = [keep.tile([P, T // PER_COL], U16, name=f"pos_sb{r}") for r in range(TOP)]
        xw = keep.tile([P, (PASSES - 1) * T + WINDOW], U32, name="xw", align_bytes=64)
        xw_start = [2 * T, 0, T]
        xs = keep.tile([P, WINDOW], U8, name="xs", align_bytes=64)
        bias = keep.tile([P, E], F32, name="bias")
        gates = {t0: keep.tile([P, TOP, t1 - t0], F32, name=f"gates{t0}") for t0, t1 in ((0, CUT), (CUT, T))}

        nc.vector.memset(xs[:].bitcast(I32), 0)
        nc.vector.memset(xw[:, PASSES * T :].bitcast(I32), 0)
        ident = keep.tile([P, P], F32, name="ident")
        make_identity(nc, ident[:])

        raw = {}

        def load_w(e, a0, a1):
            t = keep.tile([P, a1 - a0, PACK * N], F32, name=f"raw{e}_{a0}")
            nc.sync.dma_start(out=t[:], in_=w[e].rearrange("(g p j) n -> p g (j n)", p=P, j=PACK)[:, a0:a1, :])
            raw[(e, a0)] = (t, a1 - a0)

        x_i32 = x_words.rearrange("a p t r -> p a (t r)").bitcast(I32)

        nc.sync.dma_start(offs_sb[:], offs)
        for e in range(E):
            if e == 0:
                nc.scalar.dma_start(out=xw[:, 2 * T : 3 * T].bitcast(I32), in_=x_i32[:, 0, :])
            if e == 1:
                nc.sync.dma_start(out=xw[:, : 2 * T].bitcast(I32).rearrange("p (a t) -> p a t", t=T), in_=x_i32[:, 1:, :])
            if e in BY_PASS:
                for a in range(PASSES):
                    load_w(e, a, a + 1)
            else:
                load_w(e, 0, PASSES)
            if e == SCALES_AFTER:
                for q in range(4):
                    nc.sync.dma_start(out=xs[32 * q : 32 * q + 4 * PASSES, :T].bitcast(I32), in_=x_scales[:, 4 * q : 4 * q + 4, :].bitcast(I32))
            if e == BIAS_AFTER:
                nc.sync.dma_start(out=bias[:], in_=b)
        for r, pos in enumerate((pos1, pos2, pos3)):
            nc.sync.dma_start(pos_sb[r][:], pos)
        for t0, t1 in ((0, CUT), (CUT, T)):
            nc.sync.dma_start(out=gates[t0][:], in_=gate[:, :, t0:t1].rearrange("r n t -> n r t"))

        gw = []
        for a in range(PASSES):
            gathered = keep.tile([P, SLOTS], U32, name=f"gw{a}", align_bytes=64)
            nc.vector.tensor_copy(out=gathered[:], in_=xw[:, xw_start[a] : xw_start[a] + WINDOW].indirect(offs_sb[:]))
            gw.append(gathered)
        gs = keep.tile([P, SLOTS], U8, name="gs", align_bytes=64)
        nc.vector.tensor_copy(out=gs[:], in_=xs[:].indirect(offs_sb[:]))

        y = keep.tile([P, SLOTS], F32, name="y")
        banks = [psum.tile([P, 512], F32, name=f"bank{i}") for i in range(8)]

        wb = keep.tile([P, E * PASSES, N * PACK], BF16, name="wb", align_bytes=64)
        for e in range(E):
            for a0 in range(PASSES):
                if (e, a0) not in raw:
                    continue
                t, count = raw[(e, a0)]
                src = t[:].rearrange("p g (j c i) -> p g c j i", j=PACK, i=2)
                dst = wb[:, e * PASSES + a0 : e * PASSES + a0 + count, :].rearrange("p g (c i j) -> p g c j i", j=PACK, i=2)
                on_vector = [g for g in range(count) if (e, a0 + g) in ON_VECTOR]
                for g in on_vector:
                    nc.vector.tensor_copy(out=dst[:, g], in_=src[:, g])
                if e == 0:
                    for g in range(count):
                        nc.scalar.activation(out=dst[:, g], in_=src[:, g], func=ACT.Copy)
                elif len(on_vector) < count:
                    nc.scalar.copy(out=dst[:, len(on_vector) :], in_=src[:, len(on_vector) :])

        codes = keep.tile([P, E * PASSES * N], U32, name="codes", align_bytes=64)
        scales = keep.tile([P, E * PASSES * N], U8, name="scales", align_bytes=64)
        flat = wb[:].rearrange("p g m -> p (g m)")
        accs = []
        u0 = 0
        for width in QUANTS:
            u1 = u0 + width
            nc.vector.quantize_mx(
                out=codes[:, u0 * N : u1 * N].bitcast(FP8X4),
                scales=scales[:, u0 * N : u1 * N],
                in_=flat[:, u0 * N * PACK : u1 * N * PACK],
            )
            for u in range(u0, u1):
                e, a = divmod(u, PASSES)
                bank, place = BANK_OF[e]
                acc = banks[bank][:, place * C : (place + 1) * C]
                nc.tensor.matmul_mx(
                    out=acc,
                    lhsT=codes[:, u * N : (u + 1) * N].bitcast(FP8X4),
                    lhsT_scale=scales[:, u * N : (u + 1) * N],
                    rhs=gw[a][:, e * C : (e + 1) * C].bitcast(FP8X4),
                    rhs_scale=gs[4 * a : P, e * C : (e + 1) * C],
                    start=(a == 0),
                    stop=(a == PASSES - 1),
                )
                if a == 0:
                    accs.append(acc)
            u0 = u1

        rel = keep.tile([P, SLOTS], F32, name="rel")
        for e0, e1 in SQUARES:
            for e in range(e0, e1):
                nc.scalar.activation(out=rel[:, e * C : (e + 1) * C], in_=accs[e], func=ACT.Relu, bias=bias[:, e : e + 1])
            nc.scalar.activation(out=y[:, e0 * C : e1 * C], in_=rel[:, e0 * C : e1 * C], func=ACT.Square)

        cols = slice((E - 1) * C, E * C)
        nc.vector.tensor_scalar(out=rel[:, cols], in0=accs[E - 1], scalar1=bias[:, E - 1 :], scalar2=0.0, op0=ALU.add, op1=ALU.max)
        nc.vector.tensor_tensor(out=y[:, cols], in0=rel[:, cols], in1=rel[:, cols], op=ALU.mult)

        def weigh(t0, t1, r):
            term = keep.tile([P, t1 - t0], F32, name=f"term{t0}_{r}")
            nc.vector.tensor_tensor(out=term[:], in0=y[:].indirect(pos_sb[r][:, t0 // PER_COL : t1 // PER_COL]), in1=gates[t0][:, r, :], op=ALU.mult)
            return term

        def add(left, right, name):
            total = keep.tile(list(left.shape), F32, name=name)
            nc.vector.tensor_tensor(out=total[:], in0=left[:], in1=right[:], op=ALU.add)
            return total

        first = [weigh(0, CUT, r) for r in range(TOP)]
        turned = keep.tile([P, CUT], F32, name="turned")
        first_sum = keep.tile([P, CUT], F32, name="first_sum")
        blocks = [slice(t0, t0 + P) for t0 in range(0, CUT, P)]
        for r in range(TOP):
            for i, cols in enumerate(blocks):
                nc.tensor.matmul(banks[i][:, :P], lhsT=first[r][:, cols], rhs=ident[:], is_transpose=True, start=(r == 0), stop=(r == TOP - 1))
        for i, cols in enumerate(blocks):
            nc.scalar.copy(out=turned[:, cols], in_=banks[i][:, :P])
            nc.tensor.transpose(banks[len(blocks) + i][:, :P], turned[:, cols], ident[:])
        for i, cols in enumerate(blocks):
            nc.scalar.copy(out=first_sum[:, cols], in_=banks[len(blocks) + i][:, :P])
        nc.sync.dma_start(out=out[:, :CUT], in_=first_sum[:])
        last = [weigh(CUT, T, r) for r in range(TOP)]
        last_two = add(last[0], last[1], "last_two")
        last_sum = add(last_two, last[2], "last_sum")
        nc.sync.dma_start(out=out[:, CUT:], in_=last_sum[:])
